import numpy as np
import ml_dtypes


def mxq(x, axis, fmt="e4m3"):
    dtype, down = {"e4m3": (ml_dtypes.float8_e4m3fn, 7), "e5m2": (ml_dtypes.float8_e5m2, 14)}[fmt]
    v = np.moveaxis(np.asarray(x, np.float32).astype(ml_dtypes.bfloat16).astype(np.float64), axis, -1)
    blocks = v.reshape(v.shape[:-1] + (-1, 32))
    amax = np.abs(blocks).max(-1, keepdims=True)
    byte = np.maximum(np.where(amax > 0, np.frexp(amax)[1] - 1 + 127, 0) - down, 1)
    scale = np.exp2(byte - 127.0)
    codes = (blocks / scale).astype(np.float32).astype(dtype).astype(np.float64)
    return np.moveaxis((codes * scale).reshape(v.shape), -1, axis)


WIDE = False


def mx_kscale(k):
    if not WIDE:
        return np.ones(k)
    levels = np.array([10, -10, 5, -5, 0])
    if k % 512:
        return np.exp2(np.random.permutation(np.resize(levels, k // 32))).repeat(32)
    a = np.empty((k // 512, 16))
    for p in range(k // 512):
        a[p, :8] = np.random.permutation(np.resize(levels, 8))
        for g in range(8):
            far = levels[np.abs(levels - a[p, g]) >= 10]
            a[p, g + 8] = far[np.random.randint(len(far))]
    return np.exp2(a.ravel()).repeat(32)


def f64(x):
    return np.asarray(x).astype(np.float64)


def striped(idx):
    return np.tile(np.asarray(idx).reshape(-1, 16).T, (8, 1)).astype(np.uint16)


def unstriped(offs):
    return offs[:16].T.reshape(-1).astype(np.int64)


E2M1 = np.array([0.0, 0.5, 1.0, 1.5, 2.0, 3.0, 4.0, 6.0, -0.0, -0.5, -1.0, -1.5, -2.0, -3.0, -4.0, -6.0])


def pack_weight(w, fmt):
    k, n = w.shape
    w = f64(np.asarray(w, np.float32).astype(ml_dtypes.bfloat16)).reshape(k // 32, 32, n)
    amax = np.abs(w).max(1)
    if fmt == "e4m3":
        byte = np.frexp(amax)[1] - 1 + 127 - 7
    else:
        mant, ex = np.frexp(amax / 6.0)
        byte = np.where(mant > 0.5, ex, ex - 1) + 127
    byte = np.clip(np.where(amax > 0, byte, 1), 1, 254)
    scaled = (w * np.exp2(127.0 - byte)[:, None, :]).reshape(k, n).astype(np.float32)
    by_word = np.ascontiguousarray(scaled.reshape(k // 512, 128, 4, n).transpose(0, 1, 3, 2))
    if fmt == "e4m3":
        words = by_word.astype(ml_dtypes.float8_e4m3fn).view(np.uint8)
    else:
        c = by_word.astype(ml_dtypes.float4_e2m1fn).view(np.uint8) & 0xF
        words = (c[..., 0::2] | (c[..., 1::2] << 4)).reshape(k // 512, 128, 2 * n)
    return np.ascontiguousarray(words), np.ascontiguousarray(byte.astype(np.uint8).reshape(k // 512, 16, n))


def unpack_weight(words, scales, fmt):
    g, _, n = scales.shape
    words = np.ascontiguousarray(words).reshape(g, 128, n, -1)
    if fmt == "e4m3":
        vals = words.view(ml_dtypes.float8_e4m3fn).astype(np.float64)
    else:
        nib = np.empty((g, 128, n, 4), np.uint8)
        nib[..., 0::2] = words & 0xF
        nib[..., 1::2] = words >> 4
        vals = E2M1[nib]
    vals = vals * np.repeat(np.exp2(scales.astype(np.float64) - 127.0), 8, axis=1)[..., None]
    return vals.transpose(0, 1, 3, 2).reshape(g * 512, n)


def sigmoid(v):
    return 1.0 / (1.0 + np.exp(-v))


K, T, J, B, N = 1024, 2048, 512, 64, 512


def setup_inputs():
    n = np.random.standard_normal
    idx = np.random.permutation(T)[:J]
    fk = mx_kscale(K)
    xtp = pack_weight(n((K, T)) / fk[:, None], "e4m3")
    wvp = pack_weight(n((K, N)) * 1 / np.sqrt(K) * fk[:, None], "e2m1")
    return {
        "xt_words": xtp[0],
        "xt_scales": xtp[1],
        "wv_words": wvp[0],
        "wv_scales": wvp[1],
        "wg": (n((K, N)) * 1 / np.sqrt(K) * fk[:, None]).astype(np.float32),
        "bw": (np.random.uniform(0.5, 2.0, (1, B))).astype(np.float32),
        "offs": striped(idx),
    }


def reference(xt_words, xt_scales, wv_words, wv_scales, wg, bw, offs):
    idx = unstriped(offs)
    xtu = unpack_weight(xt_words, xt_scales, "e4m3")
    wvu = unpack_weight(wv_words, wv_scales, "e2m1")
    xtidxg = xtu[:, idx]
    v = wvu.T @ xtidxg
    wgq = mxq(f64(wg), 0, "e4m3")
    g = wgq.T @ xtidxg
    s = sigmoid(g)
    num = (s * v).reshape(N, B, J // B).sum(axis=2)
    den = s.reshape(N, B, J // B).sum(axis=2)
    y = f64(bw) * num / (den + 0.1)
    return y

@@ -1,0 +1,187 @@
+from contextlib import ExitStack
+
+import concourse.mybir as mybir
+from concourse.masks import make_identity
+
+K, T, J, B, N = 1024, 2048, 512, 64, 512
+FLOPS = 2 * 2 * K * N * J
+
+F32 = mybir.dt.float32
+BF16 = mybir.dt.bfloat16
+I32 = mybir.dt.int32
+U32 = mybir.dt.uint32
+U16 = mybir.dt.uint16
+U8 = mybir.dt.uint8
+FP8X4 = mybir.dt.float8_e4m3fn_x4
+FP4X4 = mybir.dt.float4_e2m1fn_x4
+ACT = mybir.ActivationFunctionType
+ALU = mybir.AluOpType
+
+P = 128
+PACK = 4
+PASSES = K // (P * PACK)
+GROUP = J // B
+BLOCKS = N // P
+QUAD = 32
+ROWS = 4
+PARK = QUAD - PASSES * ROWS
+WG_LOADS = [(0, 0, 256), (1, 0, 256), (0, 256, 256), (1, 256, 128), (1, 384, 128)]
+ON_VECTOR = [(0, 1), (3, 1)]
+
+
+def tile_list_gated_mean_of_picks_kernel(tc, xt_words, xt_scales, wv_words, wv_scales, wg, bw, offs, out):
+    nc = tc.nc
+    with ExitStack() as ctx:
+        keep = ctx.enter_context(tc.tile_pool(name="keep", bufs=1))
+        psum = ctx.enter_context(tc.psum_pool(name="psum", bufs=1))
+
+        offsets = keep.tile([P, J // 16], U16, name="offsets")
+        xs_table = keep.tile([P, T], U8, name="xs_table", align_bytes=64)
+        x_table = [keep.tile([P, T], I32, name="x_table%d" % z, align_bytes=64) for z in range(PASSES)]
+        wv_codes = keep.tile([P, PASSES, 2 * N], U8, name="wv_codes", align_bytes=64)
+        wv_planes = keep.tile([P, PASSES, N], U8, name="wv_planes", align_bytes=64)
+        xs_picked = keep.tile([P, J], U8, name="xs_picked", align_bytes=64)
+        x_planes = [keep.tile([P, J], U8, name="x_plane%d" % z, align_bytes=64) for z in range(PASSES)]
+        x_picked = [keep.tile([P, J], U32, name="x_picked%d" % z, align_bytes=64) for z in range(PASSES)]
+        ident = keep.tile([P, P], F32, name="ident")
+        factor = keep.tile([P, 1], F32, name="factor")
+        is_den = keep.tile([P, 1], F32, name="is_den")
+        shift = keep.tile([P, 1], F32, name="shift")
+        warm = keep.tile([P, 1], F32, name="warm")
+
+        nc.vector.memset(wv_planes[:].rearrange("p z n -> p (z n)").bitcast(I32), 0)
+        for q in range(P // QUAD):
+            nc.vector.memset(xs_table[QUAD * q : QUAD * q + PARK, :].bitcast(I32), 0)
+        for z in range(PASSES):
+            nc.vector.memset(x_planes[z][:].bitcast(I32), 0)
+        nc.vector.memset(is_den[0:B, :], 1.0)
+        nc.vector.memset(is_den[B:P, :], 0.0)
+        nc.vector.memset(factor[0:B, :], 1.0)
+        nc.vector.tensor_scalar(shift[:], is_den[:], 0.1, None, ALU.mult)
+        nc.scalar.activation(warm[:], is_den[:], ACT.Sigmoid)
+
+        def load_x(z):
+            nc.sync.dma_start(x_table[z][:], xt_words[z].rearrange("p t r -> p (t r)").bitcast(I32))
+
+        raw = {}
+
+        def load_wg(z, c0, width):
+            tile = keep.tile([P, PACK, width], F32, name="wg_raw_%d_%d" % (z, c0))
+            rows = wg[z * P * PACK : (z + 1) * P * PACK, c0 : c0 + width]
+            nc.sync.dma_start(tile[:], rows.rearrange("(p j) w -> p j w", j=PACK))
+            for c in range(c0, c0 + width, P):
+                raw[(c // P, z)] = tile[:, :, c - c0 : c - c0 + P]
+
+        for q in range(P // QUAD):
+            nc.sync.dma_start(
+                xs_table[QUAD * q + PARK : QUAD * (q + 1), :].bitcast(I32),
+                xt_scales[:, ROWS * q : ROWS * (q + 1), :].bitcast(I32),
+            )
+        nc.sync.dma_start(offsets[:], offs)
+        load_x(0)
+        nc.sync.dma_start(wv_codes[:].bitcast(I32), wv_words.rearrange("z p c -> p z c").bitcast(I32))
+        for q in range(0, 1):
+            nc.sync.dma_start(
+                wv_planes[QUAD * q : QUAD * q + ROWS, :, :].bitcast(I32),
+                wv_scales[:, ROWS * q : ROWS * (q + 1), :].rearrange("z r n -> r z n").bitcast(I32),
+            )
+        load_x(1)
+        for q in range(1, 4):
+            nc.sync.dma_start(
+                wv_planes[QUAD * q : QUAD * q + ROWS, :, :].bitcast(I32),
+                wv_scales[:, ROWS * q : ROWS * (q + 1), :].rearrange("z r n -> r z n").bitcast(I32),
+            )
+        for z, c0, width in WG_LOADS[0:5]:
+            load_wg(z, c0, width)
+        with nc.allow_non_contiguous_dma(reason="one group weight a partition"):
+            nc.sync.dma_start(factor[B:P, :], bw.rearrange("o b -> b o"))
+
+        make_identity(nc, ident[:])
+        nc.vector.tensor_copy(xs_picked[:], xs_table[:].indirect(offsets[:]))
+        for z in range(PASSES):
+            first = PARK + ROWS * z
+            count = P - QUAD + ROWS
+            nc.scalar.dma_start(x_planes[z][0:count, :].bitcast(I32), xs_picked[first : first + count, :].bitcast(I32))
+
+        g_bank = [psum.tile([P, J], F32, name="g_bank%d" % nb) for nb in range(BLOCKS)]
+        v_bank = [psum.tile([P, J], F32, name="v_bank%d" % nb) for nb in range(BLOCKS)]
+
+        def pick(z):
+            nc.vector.tensor_copy(x_picked[z][:], x_table[z][:].bitcast(U32).indirect(offsets[:]))
+
+        def v_pass(nb, z):
+            nc.tensor.matmul_mx(
+                v_bank[nb][:],
+                lhsT=wv_codes[:, z, 2 * P * nb : 2 * P * (nb + 1)].bitcast(FP4X4),
+                lhsT_scale=wv_planes[:, z, P * nb : P * (nb + 1)],
+                rhs=x_picked[z][:].bitcast(FP8X4),
+                rhs_scale=x_planes[z][:],
+                start=(z == 0),
+                stop=(z == PASSES - 1),
+            )
+
+        def quantize(nb, z):
+            grouped = keep.tile([P, P, PACK], BF16, name="grouped_%d_%d" % (nb, z), align_bytes=64)
+            src = raw[(nb, z)].rearrange("p j w -> p w j")
+            if (nb, z) in ON_VECTOR:
+                nc.vector.tensor_copy(grouped[:], src)
+            else:
+                nc.scalar.copy(grouped[:], src)
+            codes = keep.tile([P, P], U32, name="wg_codes_%d_%d" % (nb, z), align_bytes=64)
+            plane = keep.tile([P, P], U8, name="wg_plane_%d_%d" % (nb, z), align_bytes=64)
+            nc.vector.quantize_mx(codes[:].bitcast(FP8X4), plane[:], grouped[:].rearrange("p w j -> p (w j)"))
+            return codes, plane
+
+        def g_pass(nb, z, codes, plane):
+            nc.tensor.matmul_mx(
+                g_bank[nb][:],
+                lhsT=codes[:].bitcast(FP8X4),
+                lhsT_scale=plane[:],
+                rhs=x_picked[z][:].bitcast(FP8X4),
+                rhs_scale=x_planes[z][:],
+                start=(z == 0),
+                stop=(z == PASSES - 1),
+            )
+
+        def finish(nb):
+            parts = 2
+            step = GROUP // parts
+            g_by_slot = g_bank[nb][:].rearrange("p (b i) -> p i b", i=GROUP)
+            v_by_slot = v_bank[nb][:].rearrange("p (b i) -> p i b", i=GROUP)
+            terms = [keep.tile([P, step, 2, B], F32, name="terms_%d_%d" % (nb, h)) for h in range(parts)]
+            for h in range(parts):
+                nc.scalar.activation(terms[h][:, :, 0, :], g_by_slot[:, h * step : (h + 1) * step, :], ACT.Sigmoid)
+            for h in range(parts):
+                nc.vector.tensor_tensor(
+                    terms[h][:, :, 1, :], v_by_slot[:, h * step : (h + 1) * step, :], terms[h][:, :, 0, :], ALU.mult
+                )
+            sums_t = g_bank[nb][:, 0:P]
+            for i in range(GROUP):
+                nc.tensor.matmul(
+                    sums_t,
+                    lhsT=terms[i // step][:, i % step, :, :].rearrange("p c b -> p (c b)"),
+                    rhs=ident[:],
+                    is_transpose=True,
+                    start=(i == 0),
+                    stop=(i == GROUP - 1),
+                )
+            scaled_t = keep.tile([P, P], F32, name="scaled_t%d" % nb)
+            nc.scalar.activation(scaled_t[:], sums_t, ACT.Identity, bias=shift[:], scale=factor[:])
+            sums = v_bank[nb][:, 0:P]
+            nc.tensor.transpose(sums, scaled_t[:], ident[:])
+            inverse = keep.tile([P, B], F32, name="inverse%d" % nb)
+            nc.vector.reciprocal(inverse[:], sums[:, 0:B])
+            result = keep.tile([P, B], F32, name="result%d" % nb)
+            nc.vector.tensor_tensor(result[:], sums[:, B:P], inverse[:], ALU.mult)
+            nc.sync.dma_start(out[P * nb : P * (nb + 1), :], result[:])
+
+        pick(0)
+        for nb in range(BLOCKS):
+            v_pass(nb, 0)
+        pick(1)
+        for nb in range(BLOCKS):
+            for z in range(PASSES):
+                codes, plane = quantize(nb, z)
+                g_pass(nb, z, codes, plane)
+            v_pass(nb, 1)
+            finish(nb)

@@ -16,17 +16,22 @@ FP8X4 = mybir.dt.float8_e4m3fn_x4
 FP4X4 = mybir.dt.float4_e2m1fn_x4
 ACT = mybir.ActivationFunctionType
 ALU = mybir.AluOpType
+AXIS = mybir.AxisListType
 
 P = 128
 PACK = 4
 PASSES = K // (P * PACK)
 GROUP = J // B
+CHUNKS = J // P
+HALVES = GROUP // CHUNKS
 BLOCKS = N // P
 QUAD = 32
 ROWS = 4
-PARK = QUAD - PASSES * ROWS
-WG_LOADS = [(0, 0, 256), (1, 0, 256), (0, 256, 256), (1, 256, 128), (1, 384, 128)]
-ON_VECTOR = [(0, 1), (3, 1)]
+MOVED = 112
+WG_FIRST = [(0, 0, 128)]
+WG_LOADS = [(1, 0, 128)] + [(z, c0, 128) for c0 in (128, 256, 384) for z in (0, 1)]
+ON_VECTOR = [(3, 1)]
+PARTS = 2
 
 
 def tile_list_gated_mean_of_picks_kernel(tc, xt_words, xt_scales, wv_words, wv_scales, wg, bw, offs, out):
@@ -36,91 +41,102 @@ def tile_list_gated_mean_of_picks_kernel(tc, xt_words, xt_scales, wv_words, wv_s
         psum = ctx.enter_context(tc.psum_pool(name="psum", bufs=1))
 
         offsets = keep.tile([P, J // 16], U16, name="offsets")
-        xs_table = keep.tile([P, T], U8, name="xs_table", align_bytes=64)
-        x_table = [keep.tile([P, T], I32, name="x_table%d" % z, align_bytes=64) for z in range(PASSES)]
+        xs_table = keep.tile([P, T], U8, name="xs_table", tag="xs_table", align_bytes=64)
         wv_codes = keep.tile([P, PASSES, 2 * N], U8, name="wv_codes", align_bytes=64)
         wv_planes = keep.tile([P, PASSES, N], U8, name="wv_planes", align_bytes=64)
-        xs_picked = keep.tile([P, J], U8, name="xs_picked", align_bytes=64)
-        x_planes = [keep.tile([P, J], U8, name="x_plane%d" % z, align_bytes=64) for z in range(PASSES)]
-        x_picked = [keep.tile([P, J], U32, name="x_picked%d" % z, align_bytes=64) for z in range(PASSES)]
+        xs_picked = keep.tile([P, J], U8, name="xs_picked", tag="staging", align_bytes=64)
+        xs_dealt = keep.tile([P, J], U8, name="xs_dealt", align_bytes=64)
+        xs_lowered = keep.tile([P, J], U8, name="xs_lowered", align_bytes=64)
+        x_picked = [keep.tile([P, CHUNKS, P], U32, name="x_picked%d" % z, align_bytes=64) for z in range(PASSES)]
         ident = keep.tile([P, P], F32, name="ident")
-        factor = keep.tile([P, 1], F32, name="factor")
-        is_den = keep.tile([P, 1], F32, name="is_den")
-        shift = keep.tile([P, 1], F32, name="shift")
+        one = keep.tile([P, 1], F32, name="one", tag="tables", align_bytes=64)
+        share = keep.tile([P, 1], F32, name="share")
         warm = keep.tile([P, 1], F32, name="warm")
 
-        nc.vector.memset(wv_planes[:].rearrange("p z n -> p (z n)").bitcast(I32), 0)
-        for q in range(P // QUAD):
-            nc.vector.memset(xs_table[QUAD * q : QUAD * q + PARK, :].bitcast(I32), 0)
-        for z in range(PASSES):
-            nc.vector.memset(x_planes[z][:].bitcast(I32), 0)
-        nc.vector.memset(is_den[0:B, :], 1.0)
-        nc.vector.memset(is_den[B:P, :], 0.0)
-        nc.vector.memset(factor[0:B, :], 1.0)
-        nc.vector.tensor_scalar(shift[:], is_den[:], 0.1, None, ALU.mult)
-        nc.scalar.activation(warm[:], is_den[:], ACT.Sigmoid)
+        nc.vector.memset(xs_table[:, 0 : T // 2].bitcast(I32), 0)
+        nc.gpsimd.memset(xs_table[:, T // 2 : T].bitcast(I32), 0)
+        nc.vector.memset(one[:], 1.0)
+        nc.vector.tensor_scalar(share[:], one[:], 0.1, None, ALU.mult)
+        nc.scalar.activation(warm[:], share[:], ACT.Sigmoid)
+        nc.gpsimd.memset(wv_planes[:].rearrange("p z n -> p (z n)").bitcast(I32), 0)
+        nc.gpsimd.memset(xs_lowered[:].bitcast(I32), 0)
+        make_identity(nc, ident[:])
+        tables = keep.tile([P, PASSES * T], I32, name="tables", tag="tables", align_bytes=64)
+        x_table = [tables[:, z * T : (z + 1) * T] for z in range(PASSES)]
 
         def load_x(z):
-            nc.sync.dma_start(x_table[z][:], xt_words[z].rearrange("p t r -> p (t r)").bitcast(I32))
+            nc.sync.dma_start(x_table[z], xt_words[z].rearrange("p t r -> p (t r)").bitcast(I32))
 
         raw = {}
+        spent = {}
 
-        def load_wg(z, c0, width):
-            tile = keep.tile([P, PACK, width], F32, name="wg_raw_%d_%d" % (z, c0))
-            rows = wg[z * P * PACK : (z + 1) * P * PACK, c0 : c0 + width]
-            nc.sync.dma_start(tile[:], rows.rearrange("(p j) w -> p j w", j=PACK))
-            for c in range(c0, c0 + width, P):
-                raw[(c // P, z)] = tile[:, :, c - c0 : c - c0 + P]
+        def load_wg(staged, loads):
+            at = 0
+            for z, c0, width in loads:
+                piece = staged[:, at : at + PACK * width].rearrange("p (j w) -> p j w", j=PACK)
+                rows = wg[z * P * PACK : (z + 1) * P * PACK, c0 : c0 + width]
+                nc.sync.dma_start(piece, rows.rearrange("(p j) w -> p j w", j=PACK))
+                for c in range(c0, c0 + width, P):
+                    raw[(c // P, z)] = piece[:, :, c - c0 : c - c0 + P]
+                    spent[(c // P, z)] = staged[:, at : at + PACK * width]
+                at = at + PACK * width
 
+        nc.sync.dma_start(offsets[:], offs)
+        wg_first = keep.tile([P, PACK * sum(w for z, c0, w in WG_FIRST)], F32, name="wg_first", align_bytes=64)
+        load_wg(wg_first, WG_FIRST)
+        nc.sync.dma_start(wv_codes[:].bitcast(I32), wv_words.rearrange("z p c -> p z c").bitcast(I32))
         for q in range(P // QUAD):
             nc.sync.dma_start(
-                xs_table[QUAD * q + PARK : QUAD * (q + 1), :].bitcast(I32),
+                xs_table[QUAD * q : QUAD * q + PASSES * ROWS, :].bitcast(I32),
                 xt_scales[:, ROWS * q : ROWS * (q + 1), :].bitcast(I32),
             )
-        nc.sync.dma_start(offsets[:], offs)
         load_x(0)
-        nc.sync.dma_start(wv_codes[:].bitcast(I32), wv_words.rearrange("z p c -> p z c").bitcast(I32))
-        for q in range(0, 1):
+        for q in range(P // QUAD):
             nc.sync.dma_start(
                 wv_planes[QUAD * q : QUAD * q + ROWS, :, :].bitcast(I32),
                 wv_scales[:, ROWS * q : ROWS * (q + 1), :].rearrange("z r n -> r z n").bitcast(I32),
             )
         load_x(1)
-        for q in range(1, 4):
-            nc.sync.dma_start(
-                wv_planes[QUAD * q : QUAD * q + ROWS, :, :].bitcast(I32),
-                wv_scales[:, ROWS * q : ROWS * (q + 1), :].rearrange("z r n -> r z n").bitcast(I32),
-            )
-        for z, c0, width in WG_LOADS[0:5]:
-            load_wg(z, c0, width)
-        with nc.allow_non_contiguous_dma(reason="one group weight a partition"):
-            nc.sync.dma_start(factor[B:P, :], bw.rearrange("o b -> b o"))
 
-        make_identity(nc, ident[:])
         nc.vector.tensor_copy(xs_picked[:], xs_table[:].indirect(offsets[:]))
-        for z in range(PASSES):
-            first = PARK + ROWS * z
-            count = P - QUAD + ROWS
-            nc.scalar.dma_start(x_planes[z][0:count, :].bitcast(I32), xs_picked[first : first + count, :].bitcast(I32))
+        weight = keep.tile([P, 1], F32, name="weight", tag="xs_table", align_bytes=64)
+        with nc.allow_non_contiguous_dma(reason="one group weight a partition"):
+            for h in range(HALVES):
+                nc.sync.dma_start(weight[h:P:HALVES, :], bw.rearrange("o b -> b o"))
+        nc.vector.tensor_copy(
+            xs_dealt[:].rearrange("q (c p) -> q c p", c=CHUNKS), xs_picked[:].rearrange("q (p c) -> q c p", c=CHUNKS)
+        )
+        nc.sync.dma_start(xs_lowered[0:MOVED, :].bitcast(I32), xs_dealt[ROWS : ROWS + MOVED, :].bitcast(I32))
+        wg_rest = keep.tile(
+            [P, PACK * sum(w for z, c0, w in WG_LOADS)], F32, name="wg_rest", tag="staging", align_bytes=64
+        )
+        load_wg(wg_rest, WG_LOADS)
 
         g_bank = [psum.tile([P, J], F32, name="g_bank%d" % nb) for nb in range(BLOCKS)]
         v_bank = [psum.tile([P, J], F32, name="v_bank%d" % nb) for nb in range(BLOCKS)]
 
         def pick(z):
-            nc.vector.tensor_copy(x_picked[z][:], x_table[z][:].bitcast(U32).indirect(offsets[:]))
-
-        def v_pass(nb, z):
-            nc.tensor.matmul_mx(
-                v_bank[nb][:],
-                lhsT=wv_codes[:, z, 2 * P * nb : 2 * P * (nb + 1)].bitcast(FP4X4),
-                lhsT_scale=wv_planes[:, z, P * nb : P * (nb + 1)],
-                rhs=x_picked[z][:].bitcast(FP8X4),
-                rhs_scale=x_planes[z][:],
-                start=(z == 0),
-                stop=(z == PASSES - 1),
+            nc.vector.tensor_copy(
+                x_picked[z][:].rearrange("q c p -> q p c"), x_table[z].bitcast(U32).indirect(offsets[:])
             )
 
-        def quantize(nb, z):
+        def passes(bank, z, x_plane, codes, plane):
+            for c in range(CHUNKS):
+                nc.tensor.matmul_mx(
+                    bank[:, P * c : P * (c + 1)],
+                    lhsT=x_picked[z][:, c, :].bitcast(FP8X4),
+                    lhsT_scale=x_plane[:, P * c : P * (c + 1)],
+                    rhs=codes,
+                    rhs_scale=plane,
+                    start=(z == 0 and c == 0),
+                    stop=(z == PASSES - 1 and c == CHUNKS - 1),
+                )
+
+        def v_passes(nb, z):
+            codes = wv_codes[:, z, 2 * P * nb : 2 * P * (nb + 1)].bitcast(FP4X4)
+            passes(v_bank[nb], z, xs_dealt[:] if z == 0 else xs_lowered[:], codes, wv_planes[:, z, P * nb : P * (nb + 1)])
+
+        def g_passes(nb, z):
             grouped = keep.tile([P, P, PACK], BF16, name="grouped_%d_%d" % (nb, z), align_bytes=64)
             src = raw[(nb, z)].rearrange("p j w -> p w j")
             if (nb, z) in ON_VECTOR:
@@ -130,58 +146,56 @@ def tile_list_gated_mean_of_picks_kernel(tc, xt_words, xt_scales, wv_words, wv_s
             codes = keep.tile([P, P], U32, name="wg_codes_%d_%d" % (nb, z), align_bytes=64)
             plane = keep.tile([P, P], U8, name="wg_plane_%d_%d" % (nb, z), align_bytes=64)
             nc.vector.quantize_mx(codes[:].bitcast(FP8X4), plane[:], grouped[:].rearrange("p w j -> p (w j)"))
-            return codes, plane
-
-        def g_pass(nb, z, codes, plane):
-            nc.tensor.matmul_mx(
-                g_bank[nb][:],
-                lhsT=codes[:].bitcast(FP8X4),
-                lhsT_scale=plane[:],
-                rhs=x_picked[z][:].bitcast(FP8X4),
-                rhs_scale=x_planes[z][:],
-                start=(z == 0),
-                stop=(z == PASSES - 1),
-            )
+            passes(g_bank[nb], z, xs_dealt[ROWS * z : P, :], codes[:].bitcast(FP8X4), plane[:])
 
         def finish(nb):
-            parts = 2
-            step = GROUP // parts
-            g_by_slot = g_bank[nb][:].rearrange("p (b i) -> p i b", i=GROUP)
-            v_by_slot = v_bank[nb][:].rearrange("p (b i) -> p i b", i=GROUP)
-            terms = [keep.tile([P, step, 2, B], F32, name="terms_%d_%d" % (nb, h)) for h in range(parts)]
-            for h in range(parts):
-                nc.scalar.activation(terms[h][:, :, 0, :], g_by_slot[:, h * step : (h + 1) * step, :], ACT.Sigmoid)
-            for h in range(parts):
-                nc.vector.tensor_tensor(
-                    terms[h][:, :, 1, :], v_by_slot[:, h * step : (h + 1) * step, :], terms[h][:, :, 0, :], ALU.mult
+            width = J // PARTS
+            if nb + 1 < BLOCKS:
+                gate = [spent[(nb + 1, 1 - h)][:, 0:width] for h in range(PARTS)]
+            else:
+                gate = [keep.tile([P, width], F32, name="gate_%d_%d" % (nb, h))[:] for h in range(PARTS)]
+            gated = [keep.tile([P, width], F32, name="gated_%d_%d" % (nb, h)) for h in range(PARTS)]
+            for h in range(PARTS):
+                nc.scalar.activation(gate[h], g_bank[nb][:, h * width : (h + 1) * width], ACT.Sigmoid)
+            for h in range(PARTS):
+                nc.vector.scalar_tensor_tensor(
+                    gated[h][:], v_bank[nb][:, h * width : (h + 1) * width], weight[:], gate[h], ALU.mult, ALU.mult
                 )
-            sums_t = g_bank[nb][:, 0:P]
-            for i in range(GROUP):
-                nc.tensor.matmul(
-                    sums_t,
-                    lhsT=terms[i // step][:, i % step, :, :].rearrange("p c b -> p (c b)"),
-                    rhs=ident[:],
-                    is_transpose=True,
-                    start=(i == 0),
-                    stop=(i == GROUP - 1),
-                )
-            scaled_t = keep.tile([P, P], F32, name="scaled_t%d" % nb)
-            nc.scalar.activation(scaled_t[:], sums_t, ACT.Identity, bias=shift[:], scale=factor[:])
-            sums = v_bank[nb][:, 0:P]
-            nc.tensor.transpose(sums, scaled_t[:], ident[:])
+
+            def turn_and_add(sums, terms):
+                for i, term in enumerate(terms):
+                    nc.tensor.matmul(
+                        sums, lhsT=term, rhs=ident[:], is_transpose=True, start=(i == 0), stop=(i == len(terms) - 1)
+                    )
+
+            def chunks(tiles):
+                return [tiles[c * P // width][:, c * P % width : c * P % width + P] for c in range(CHUNKS)]
+
+            den_halves = g_bank[nb][:, 0:P]
+            turn_and_add(den_halves, chunks(gate))
+            num_halves = v_bank[nb][:, 0:P]
+            turn_and_add(num_halves, chunks(gated))
+            den = keep.tile([P, B], F32, name="den%d" % nb)
+            den_first = keep.tile([P, B], F32, name="den_first%d" % nb)
+            nc.scalar.activation(den_first[:], den_halves[:, 0:P:HALVES], ACT.Identity, bias=share[:])
+            nc.vector.tensor_tensor(den[:], den_halves[:, 1:P:HALVES], den_first[:], ALU.add)
             inverse = keep.tile([P, B], F32, name="inverse%d" % nb)
-            nc.vector.reciprocal(inverse[:], sums[:, 0:B])
+            nc.vector.reciprocal(inverse[:], den[:])
+            num = keep.tile([P, B], F32, name="num%d" % nb)
+            nc.vector.tensor_reduce(num[:], num_halves.rearrange("n (b h) -> n b h", h=HALVES), AXIS.X, ALU.add)
             result = keep.tile([P, B], F32, name="result%d" % nb)
-            nc.vector.tensor_tensor(result[:], sums[:, B:P], inverse[:], ALU.mult)
+            nc.vector.tensor_tensor(result[:], num[:], inverse[:], ALU.mult)
             nc.sync.dma_start(out[P * nb : P * (nb + 1), :], result[:])
 
         pick(0)
         for nb in range(BLOCKS):
-            v_pass(nb, 0)
+            v_passes(nb, 0)
+        g_passes(0, 0)
         pick(1)
+        g_passes(0, 1)
         for nb in range(BLOCKS):
-            for z in range(PASSES):
-                codes, plane = quantize(nb, z)
-                g_pass(nb, z, codes, plane)
-            v_pass(nb, 1)
+            v_passes(nb, 1)
+            if nb + 1 < BLOCKS:
+                for z in range(PASSES):
+                    g_passes(nb + 1, z)
             finish(nb)

from contextlib import ExitStack

import concourse.mybir as mybir
from concourse.masks import make_identity

K, T, J, B, N = 1024, 2048, 512, 64, 512
FLOPS = 2 * 2 * K * N * J

F32 = mybir.dt.float32
BF16 = mybir.dt.bfloat16
I32 = mybir.dt.int32
U32 = mybir.dt.uint32
U16 = mybir.dt.uint16
U8 = mybir.dt.uint8
FP8X4 = mybir.dt.float8_e4m3fn_x4
FP4X4 = mybir.dt.float4_e2m1fn_x4
ACT = mybir.ActivationFunctionType
ALU = mybir.AluOpType
AXIS = mybir.AxisListType

P = 128
PACK = 4
PASSES = K // (P * PACK)
GROUP = J // B
CHUNKS = J // P
HALVES = GROUP // CHUNKS
BLOCKS = N // P
QUAD = 32
ROWS = 4
MOVED = 112
WG_FIRST = [(0, 0, 128)]
WG_LOADS = [(1, 0, 128)] + [(z, c0, 128) for c0 in (128, 256, 384) for z in (0, 1)]
ON_VECTOR = [(3, 1)]
PARTS = 2


def tile_list_gated_mean_of_picks_kernel(tc, xt_words, xt_scales, wv_words, wv_scales, wg, bw, offs, out):
    nc = tc.nc
    with ExitStack() as ctx:
        keep = ctx.enter_context(tc.tile_pool(name="keep", bufs=1))
        psum = ctx.enter_context(tc.psum_pool(name="psum", bufs=1))

        offsets = keep.tile([P, J // 16], U16, name="offsets")
        xs_table = keep.tile([P, T], U8, name="xs_table", tag="xs_table", align_bytes=64)
        wv_codes = keep.tile([P, PASSES, 2 * N], U8, name="wv_codes", align_bytes=64)
        wv_planes = keep.tile([P, PASSES, N], U8, name="wv_planes", align_bytes=64)
        xs_picked = keep.tile([P, J], U8, name="xs_picked", tag="staging", align_bytes=64)
        xs_dealt = keep.tile([P, J], U8, name="xs_dealt", align_bytes=64)
        xs_lowered = keep.tile([P, J], U8, name="xs_lowered", align_bytes=64)
        x_picked = [keep.tile([P, CHUNKS, P], U32, name="x_picked%d" % z, align_bytes=64) for z in range(PASSES)]
        ident = keep.tile([P, P], F32, name="ident")
        one = keep.tile([P, 1], F32, name="one", tag="tables", align_bytes=64)
        share = keep.tile([P, 1], F32, name="share")
        warm = keep.tile([P, 1], F32, name="warm")

        nc.vector.memset(xs_table[:, 0 : T // 2].bitcast(I32), 0)
        nc.gpsimd.memset(xs_table[:, T // 2 : T].bitcast(I32), 0)
        nc.vector.memset(one[:], 1.0)
        nc.vector.tensor_scalar(share[:], one[:], 0.1, None, ALU.mult)
        nc.scalar.activation(warm[:], share[:], ACT.Sigmoid)
        nc.gpsimd.memset(wv_planes[:].rearrange("p z n -> p (z n)").bitcast(I32), 0)
        nc.gpsimd.memset(xs_lowered[:].bitcast(I32), 0)
        make_identity(nc, ident[:])
        tables = keep.tile([P, PASSES * T], I32, name="tables", tag="tables", align_bytes=64)
        x_table = [tables[:, z * T : (z + 1) * T] for z in range(PASSES)]

        def load_x(z):
            nc.sync.dma_start(x_table[z], xt_words[z].rearrange("p t r -> p (t r)").bitcast(I32))

        raw = {}
        spent = {}

        def load_wg(staged, loads):
            at = 0
            for z, c0, width in loads:
                piece = staged[:, at : at + PACK * width].rearrange("p (j w) -> p j w", j=PACK)
                rows = wg[z * P * PACK : (z + 1) * P * PACK, c0 : c0 + width]
                nc.sync.dma_start(piece, rows.rearrange("(p j) w -> p j w", j=PACK))
                for c in range(c0, c0 + width, P):
                    raw[(c // P, z)] = piece[:, :, c - c0 : c - c0 + P]
                    spent[(c // P, z)] = staged[:, at : at + PACK * width]
                at = at + PACK * width

        nc.sync.dma_start(offsets[:], offs)
        wg_first = keep.tile([P, PACK * sum(w for z, c0, w in WG_FIRST)], F32, name="wg_first", align_bytes=64)
        load_wg(wg_first, WG_FIRST)
        nc.sync.dma_start(wv_codes[:].bitcast(I32), wv_words.rearrange("z p c -> p z c").bitcast(I32))
        for q in range(P // QUAD):
            nc.sync.dma_start(
                xs_table[QUAD * q : QUAD * q + PASSES * ROWS, :].bitcast(I32),
                xt_scales[:, ROWS * q : ROWS * (q + 1), :].bitcast(I32),
            )
        load_x(0)
        for q in range(P // QUAD):
            nc.sync.dma_start(
                wv_planes[QUAD * q : QUAD * q + ROWS, :, :].bitcast(I32),
                wv_scales[:, ROWS * q : ROWS * (q + 1), :].rearrange("z r n -> r z n").bitcast(I32),
            )
        load_x(1)

        nc.vector.tensor_copy(xs_picked[:], xs_table[:].indirect(offsets[:]))
        weight = keep.tile([P, 1], F32, name="weight", tag="xs_table", align_bytes=64)
        with nc.allow_non_contiguous_dma(reason="one group weight a partition"):
            for h in range(HALVES):
                nc.sync.dma_start(weight[h:P:HALVES, :], bw.rearrange("o b -> b o"))
        nc.vector.tensor_copy(
            xs_dealt[:].rearrange("q (c p) -> q c p", c=CHUNKS), xs_picked[:].rearrange("q (p c) -> q c p", c=CHUNKS)
        )
        nc.sync.dma_start(xs_lowered[0:MOVED, :].bitcast(I32), xs_dealt[ROWS : ROWS + MOVED, :].bitcast(I32))
        wg_rest = keep.tile(
            [P, PACK * sum(w for z, c0, w in WG_LOADS)], F32, name="wg_rest", tag="staging", align_bytes=64
        )
        load_wg(wg_rest, WG_LOADS)

        g_bank = [psum.tile([P, J], F32, name="g_bank%d" % nb) for nb in range(BLOCKS)]
        v_bank = [psum.tile([P, J], F32, name="v_bank%d" % nb) for nb in range(BLOCKS)]

        def pick(z):
            nc.vector.tensor_copy(
                x_picked[z][:].rearrange("q c p -> q p c"), x_table[z].bitcast(U32).indirect(offsets[:])
            )

        def passes(bank, z, x_plane, codes, plane):
            for c in range(CHUNKS):
                nc.tensor.matmul_mx(
                    bank[:, P * c : P * (c + 1)],
                    lhsT=x_picked[z][:, c, :].bitcast(FP8X4),
                    lhsT_scale=x_plane[:, P * c : P * (c + 1)],
                    rhs=codes,
                    rhs_scale=plane,
                    start=(z == 0 and c == 0),
                    stop=(z == PASSES - 1 and c == CHUNKS - 1),
                )

        def v_passes(nb, z):
            codes = wv_codes[:, z, 2 * P * nb : 2 * P * (nb + 1)].bitcast(FP4X4)
            passes(v_bank[nb], z, xs_dealt[:] if z == 0 else xs_lowered[:], codes, wv_planes[:, z, P * nb : P * (nb + 1)])

        def g_passes(nb, z):
            grouped = keep.tile([P, P, PACK], BF16, name="grouped_%d_%d" % (nb, z), align_bytes=64)
            src = raw[(nb, z)].rearrange("p j w -> p w j")
            if (nb, z) in ON_VECTOR:
                nc.vector.tensor_copy(grouped[:], src)
            else:
                nc.scalar.copy(grouped[:], src)
            codes = keep.tile([P, P], U32, name="wg_codes_%d_%d" % (nb, z), align_bytes=64)
            plane = keep.tile([P, P], U8, name="wg_plane_%d_%d" % (nb, z), align_bytes=64)
            nc.vector.quantize_mx(codes[:].bitcast(FP8X4), plane[:], grouped[:].rearrange("p w j -> p (w j)"))
            passes(g_bank[nb], z, xs_dealt[ROWS * z : P, :], codes[:].bitcast(FP8X4), plane[:])

        def finish(nb):
            width = J // PARTS
            if nb + 1 < BLOCKS:
                gate = [spent[(nb + 1, 1 - h)][:, 0:width] for h in range(PARTS)]
            else:
                gate = [keep.tile([P, width], F32, name="gate_%d_%d" % (nb, h))[:] for h in range(PARTS)]
            gated = [keep.tile([P, width], F32, name="gated_%d_%d" % (nb, h)) for h in range(PARTS)]
            for h in range(PARTS):
                nc.scalar.activation(gate[h], g_bank[nb][:, h * width : (h + 1) * width], ACT.Sigmoid)
            for h in range(PARTS):
                nc.vector.scalar_tensor_tensor(
                    gated[h][:], v_bank[nb][:, h * width : (h + 1) * width], weight[:], gate[h], ALU.mult, ALU.mult
                )

            def turn_and_add(sums, terms):
                for i, term in enumerate(terms):
                    nc.tensor.matmul(
                        sums, lhsT=term, rhs=ident[:], is_transpose=True, start=(i == 0), stop=(i == len(terms) - 1)
                    )

            def chunks(tiles):
                return [tiles[c * P // width][:, c * P % width : c * P % width + P] for c in range(CHUNKS)]

            den_halves = g_bank[nb][:, 0:P]
            turn_and_add(den_halves, chunks(gate))
            num_halves = v_bank[nb][:, 0:P]
            turn_and_add(num_halves, chunks(gated))
            den = keep.tile([P, B], F32, name="den%d" % nb)
            den_first = keep.tile([P, B], F32, name="den_first%d" % nb)
            nc.scalar.activation(den_first[:], den_halves[:, 0:P:HALVES], ACT.Identity, bias=share[:])
            nc.vector.tensor_tensor(den[:], den_halves[:, 1:P:HALVES], den_first[:], ALU.add)
            inverse = keep.tile([P, B], F32, name="inverse%d" % nb)
            nc.vector.reciprocal(inverse[:], den[:])
            num = keep.tile([P, B], F32, name="num%d" % nb)
            nc.vector.tensor_reduce(num[:], num_halves.rearrange("n (b h) -> n b h", h=HALVES), AXIS.X, ALU.add)
            result = keep.tile([P, B], F32, name="result%d" % nb)
            nc.vector.tensor_tensor(result[:], num[:], inverse[:], ALU.mult)
            nc.sync.dma_start(out[P * nb : P * (nb + 1), :], result[:])

        pick(0)
        for nb in range(BLOCKS):
            v_passes(nb, 0)
        g_passes(0, 0)
        pick(1)
        g_passes(0, 1)
        for nb in range(BLOCKS):
            v_passes(nb, 1)
            if nb + 1 < BLOCKS:
                for z in range(PASSES):
                    g_passes(nb + 1, z)
            finish(nb)
